import numpy as np
import ml_dtypes


def mxq(x, axis, fmt="e4m3"):
    dtype, down = {"e4m3": (ml_dtypes.float8_e4m3fn, 7), "e5m2": (ml_dtypes.float8_e5m2, 14)}[fmt]
    v = np.moveaxis(np.asarray(x, np.float32).astype(ml_dtypes.bfloat16).astype(np.float64), axis, -1)
    blocks = v.reshape(v.shape[:-1] + (-1, 32))
    amax = np.abs(blocks).max(-1, keepdims=True)
    byte = np.maximum(np.where(amax > 0, np.frexp(amax)[1] - 1 + 127, 0) - down, 1)
    scale = np.exp2(byte - 127.0)
    codes = (blocks / scale).astype(np.float32).astype(dtype).astype(np.float64)
    return np.moveaxis((codes * scale).reshape(v.shape), -1, axis)


WIDE = False


def mx_kscale(k):
    if not WIDE:
        return np.ones(k)
    levels = np.array([10, -10, 5, -5, 0])
    if k % 512:
        return np.exp2(np.random.permutation(np.resize(levels, k // 32))).repeat(32)
    a = np.empty((k // 512, 16))
    for p in range(k // 512):
        a[p, :8] = np.random.permutation(np.resize(levels, 8))
        for g in range(8):
            far = levels[np.abs(levels - a[p, g]) >= 10]
            a[p, g + 8] = far[np.random.randint(len(far))]
    return np.exp2(a.ravel()).repeat(32)


def f64(x):
    return np.asarray(x).astype(np.float64)


def striped8(idx):
    return np.asarray(idx).reshape(8, -1, 16).transpose(0, 2, 1).reshape(128, -1).astype(np.uint16)


def unstriped8(offs):
    return offs.reshape(8, 16, -1).transpose(0, 2, 1).reshape(8, -1).astype(np.int64)


def pick8(x, idx, run):
    r = np.arange(len(x))
    return x[r[:, None], idx[r % (8 * run) // run]]


E2M1 = np.array([0.0, 0.5, 1.0, 1.5, 2.0, 3.0, 4.0, 6.0, -0.0, -0.5, -1.0, -1.5, -2.0, -3.0, -4.0, -6.0])


def pack_weight(w, fmt):
    k, n = w.shape
    w = f64(np.asarray(w, np.float32).astype(ml_dtypes.bfloat16)).reshape(k // 32, 32, n)
    amax = np.abs(w).max(1)
    if fmt == "e4m3":
        byte = np.frexp(amax)[1] - 1 + 127 - 7
    else:
        mant, ex = np.frexp(amax / 6.0)
        byte = np.where(mant > 0.5, ex, ex - 1) + 127
    byte = np.clip(np.where(amax > 0, byte, 1), 1, 254)
    scaled = (w * np.exp2(127.0 - byte)[:, None, :]).reshape(k, n).astype(np.float32)
    by_word = np.ascontiguousarray(scaled.reshape(k // 512, 128, 4, n).transpose(0, 1, 3, 2))
    if fmt == "e4m3":
        words = by_word.astype(ml_dtypes.float8_e4m3fn).view(np.uint8)
    else:
        c = by_word.astype(ml_dtypes.float4_e2m1fn).view(np.uint8) & 0xF
        words = (c[..., 0::2] | (c[..., 1::2] << 4)).reshape(k // 512, 128, 2 * n)
    return np.ascontiguousarray(words), np.ascontiguousarray(byte.astype(np.uint8).reshape(k // 512, 16, n))


def unpack_weight(words, scales, fmt):
    g, _, n = scales.shape
    words = np.ascontiguousarray(words).reshape(g, 128, n, -1)
    if fmt == "e4m3":
        vals = words.view(ml_dtypes.float8_e4m3fn).astype(np.float64)
    else:
        nib = np.empty((g, 128, n, 4), np.uint8)
        nib[..., 0::2] = words & 0xF
        nib[..., 1::2] = words >> 4
        vals = E2M1[nib]
    vals = vals * np.repeat(np.exp2(scales.astype(np.float64) - 127.0), 8, axis=1)[..., None]
    return vals.transpose(0, 1, 3, 2).reshape(g * 512, n)


D, K, T, U, X, S, I, Q = 512, 512, 1024, 1024, 1024, 1024, 512, 128


def setup_inputs():
    n = np.random.standard_normal
    idx = np.stack([np.random.permutation(T)[:I] for _ in range(8)])
    idx2 = np.stack([np.random.permutation(U)[:I] for _ in range(8)])
    idx3 = np.stack([np.random.permutation(X)[:I] for _ in range(8)])
    idx4 = np.stack([np.random.permutation(S)[:I] for _ in range(8)])
    idx5 = np.stack([np.random.permutation(T)[:I] for _ in range(8)])
    idx6 = np.stack([np.random.permutation(S)[:I] for _ in range(8)])
    fd = mx_kscale(D)
    fk = mx_kscale(K)
    wqp = pack_weight(n((D, K)) * 1.0 / np.sqrt(D) * fd[:, None] * fk, "e4m3")
    keysp = pack_weight(n((K, T)) * 1.0 / np.sqrt(K) / fk[:, None], "e4m3")
    notesp = pack_weight(n((K, U)) * 1.0 / np.sqrt(K) / fk[:, None], "e2m1")
    usersp = pack_weight(n((D, X)) * 1.0 / np.sqrt(D) * fd[:, None], "e4m3")
    shelvesp = pack_weight(n((D, S)) * 1.0 / np.sqrt(D) * fd[:, None], "e2m1")
    return {
        "states": (n((D, Q)) * 0.95 / fd[:, None]).astype(np.float32),
        "wq_words": wqp[0],
        "wq_scales": wqp[1],
        "keys_words": keysp[0],
        "keys_scales": keysp[1],
        "notes_words": notesp[0],
        "notes_scales": notesp[1],
        "users_words": usersp[0],
        "users_scales": usersp[1],
        "shelves_words": shelvesp[0],
        "shelves_scales": shelvesp[1],
        "offs": striped8(idx),
        "offs2": striped8(idx2),
        "offs3": striped8(idx3),
        "offs4": striped8(idx4),
        "offs5": striped8(idx5),
        "offs6": striped8(idx6),
    }


def reference(states, wq_words, wq_scales, keys_words, keys_scales, notes_words, notes_scales, users_words, users_scales, shelves_words, shelves_scales, offs, offs2, offs3, offs4, offs5, offs6):
    idx = unstriped8(offs)
    idx2 = unstriped8(offs2)
    idx3 = unstriped8(offs3)
    idx4 = unstriped8(offs4)
    idx5 = unstriped8(offs5)
    idx6 = unstriped8(offs6)
    wqu = unpack_weight(wq_words, wq_scales, "e4m3")
    keysu = unpack_weight(keys_words, keys_scales, "e4m3")
    notesu = unpack_weight(notes_words, notes_scales, "e2m1")
    usersu = unpack_weight(users_words, users_scales, "e4m3")
    shelvesu = unpack_weight(shelves_words, shelves_scales, "e2m1")
    statesq = mxq(f64(states), 0, "e4m3")
    qv = wqu.T @ statesq
    qvq = mxq(qv, 0, "e4m3")
    a = qvq.T @ keysu
    b = qvq.T @ notesu
    c0 = statesq.T @ usersu
    d0 = statesq.T @ shelvesu
    hi1 = np.maximum(pick8(a, idx, 16), pick8(b, idx2, 16))
    hi2 = np.maximum(pick8(c0, idx3, 16), pick8(d0, idx4, 16))
    r = np.minimum(hi1, hi2)
    f1 = np.zeros((Q, T))
    f1[np.arange(Q)[:, None], idx[np.arange(Q) % 128 // 16]] = r
    f2 = np.zeros((Q, S))
    f2[np.arange(Q)[:, None], idx4[np.arange(Q) % 128 // 16]] = r
    aa = a - f1
    dd = d0 + f2
    y = pick8(aa, idx5, 16) + pick8(dd, idx6, 16)
    return y

@@ -1,0 +1,199 @@
+from contextlib import ExitStack
+
+import concourse.mybir as mybir
+
+F32 = mybir.dt.float32
+BF16 = mybir.dt.bfloat16
+I32 = mybir.dt.int32
+U32 = mybir.dt.uint32
+U16 = mybir.dt.uint16
+U8 = mybir.dt.uint8
+FP8X4 = mybir.dt.float8_e4m3fn_x4
+FP4X4 = mybir.dt.float4_e2m1fn_x4
+ALU = mybir.AluOpType
+COPY = mybir.ActivationFunctionType.Copy
+
+P = 128
+PACK = 4
+KDIM = 512
+COLS = 1024
+SLOTS = 512
+BANK = 512
+HALF = SLOTS // 2
+LIST_HALF = HALF // 16
+EARLY = 128
+
+FLOPS = 603979776
+
+
+def tile_attend_quartet_madefour_kernel(
+    tc, states, wq_words, wq_scales, keys_words, keys_scales, notes_words, notes_scales,
+    users_words, users_scales, shelves_words, shelves_scales,
+    offs, offs2, offs3, offs4, offs5, offs6, out,
+):
+    nc = tc.nc
+    with ExitStack() as ctx:
+        sb = ctx.enter_context(tc.tile_pool(name="sb", bufs=1))
+        ps = ctx.enter_context(tc.psum_pool(name="ps", bufs=1))
+
+        scale_inputs = [("wq", wq_scales), ("users", users_scales), ("shelves", shelves_scales),
+                        ("keys", keys_scales), ("notes", notes_scales)]
+        start_of = {}
+        width = 0
+        for name, src in scale_inputs:
+            start_of[name] = width
+            width = width + src.shape[2]
+        wq_rows = sb.tile([P, KDIM], U8, name="wq_rows", align_bytes=64)
+        nc.vector.memset(wq_rows[:].bitcast(I32), 0)
+        staged = sb.tile([P, width], U8, name="staged", align_bytes=64)
+        planes = sb.tile([P, width], U8, name="planes", align_bytes=64)
+        for i, (name, src) in enumerate(scale_inputs):
+            queue = nc.scalar if i < 3 else nc.sync
+            c0 = start_of[name]
+            rows = wq_rows[0:16, :] if name == "wq" else staged[0:16, c0:c0 + src.shape[2]]
+            queue.dma_start(out=rows.bitcast(I32), in_=src[0].bitcast(I32))
+        nc.vector.memset(planes[:].bitcast(I32), 0)
+        nc.vector.tensor_copy(
+            out=staged[:, 0:KDIM].rearrange("p (t m) -> p t m", t=PACK),
+            in_=wq_rows[:].rearrange("p (m t) -> p t m", t=PACK))
+
+        states_raw = sb.tile([P, PACK, P], F32, name="states_raw")
+        nc.sync.dma_start(out=states_raw[:], in_=states.rearrange("(p j) q -> p j q", j=PACK))
+
+        def load_words(name, src, queue=nc.sync):
+            words = sb.tile([P, src.shape[1]], U8, name=name, align_bytes=64)
+            queue.dma_start(out=words[:].bitcast(I32), in_=src.bitcast(I32))
+            return words
+
+        def load_list(name, src):
+            lst = sb.tile([P, SLOTS // 16], U16, name=name)
+            nc.sync.dma_start(lst[:], src)
+            return lst
+
+        wq_raw = load_words("wq_raw", wq_words[0].rearrange("p n t -> p (n t)"))
+        users = load_words("users", users_words[0].rearrange("p n t -> p (n t)"))
+        list3 = load_list("list3", offs3)
+        for quad in range(4):
+            nc.sync.dma_start(out=planes[32 * quad:32 * quad + 4, :].bitcast(I32),
+                              in_=staged[4 * quad:4 * quad + 4, :].bitcast(I32))
+        shelves = load_words("shelves", shelves_words[0])
+        keys = load_words("keys", keys_words[0].rearrange("p n t -> p (n t)"))
+        notes = load_words("notes", notes_words[0])
+        list4 = load_list("list4", offs4)
+        list1 = load_list("list1", offs)
+        list2 = load_list("list2", offs2)
+        list5 = load_list("list5", offs5)
+        list6 = load_list("list6", offs6)
+
+        f1 = sb.tile([P, COLS], F32, name="f1")
+        f2 = sb.tile([P, COLS], F32, name="f2")
+        nc.vector.memset(f1[:], 0.0)
+        nc.vector.memset(f2[:], 0.0)
+
+        states_bf = sb.tile([P, P * PACK], BF16, name="states_bf", align_bytes=64)
+        nc.scalar.activation(
+            out=states_bf[:].rearrange("p (c i j) -> p c j i", i=4, j=PACK),
+            in_=states_raw[:].rearrange("p j (c i) -> p c j i", i=4), func=COPY)
+        wq_dealt = sb.tile([P, KDIM], U32, name="wq_dealt", align_bytes=64)
+        nc.vector.tensor_copy(
+            out=wq_dealt[:].rearrange("p (t b i) -> p b t i", t=PACK, i=4),
+            in_=wq_raw[:].bitcast(U32).rearrange("p (b i t) -> p b t i", t=PACK, i=4))
+        s_codes = sb.tile([P, P], U32, name="s_codes", align_bytes=64)
+        s_plane = sb.tile([P, P], U8, name="s_plane", align_bytes=64)
+        nc.vector.quantize_mx(out=s_codes[:].bitcast(FP8X4), scales=s_plane[:], in_=states_bf[:])
+
+        def scores(tag, codes, plane, name, words, dtype, half):
+            bank = ps.tile([P, BANK], F32, name=f"{name}{half}", tag=tag)
+            nbytes = words.shape[1] // 2
+            c0 = start_of[name] + half * BANK
+            nc.tensor.matmul_mx(
+                out=bank[:], lhsT=codes[:].bitcast(FP8X4), lhsT_scale=plane[:],
+                rhs=words[:, half * nbytes:(half + 1) * nbytes].bitcast(dtype),
+                rhs_scale=planes[:, c0:c0 + BANK], start=True, stop=True)
+            return bank
+
+        def cols(half):
+            return slice(half * BANK, (half + 1) * BANK)
+
+        a_sb = sb.tile([P, COLS], F32, name="a_sb")
+        b_sb = sb.tile([P, COLS], F32, name="b_sb")
+        c_sb = sb.tile([P, COLS], F32, name="c_sb")
+        d_sb = sb.tile([P, COLS], F32, name="d_sb")
+
+        qv_ps = ps.tile([P, BANK], F32, name="qv_ps", tag="bank7")
+        for t in range(PACK):
+            nc.tensor.matmul_mx(
+                out=qv_ps[:, t * P:(t + 1) * P],
+                lhsT=wq_dealt[:, t * P:(t + 1) * P].bitcast(FP8X4), lhsT_scale=planes[:, t * P:(t + 1) * P],
+                rhs=s_codes[:].bitcast(FP8X4), rhs_scale=s_plane[:], start=True, stop=True)
+        c_ps0 = scores("bank0", s_codes, s_plane, "users", users, FP8X4, 0)
+        c_ps1 = scores("bank1", s_codes, s_plane, "users", users, FP8X4, 1)
+        d_ps0 = scores("bank2", s_codes, s_plane, "shelves", shelves, FP4X4, 0)
+        d_ps1 = scores("bank3", s_codes, s_plane, "shelves", shelves, FP4X4, 1)
+
+        qv_bf = sb.tile([P, P * PACK], BF16, name="qv_bf", align_bytes=64)
+        nc.scalar.activation(
+            out=qv_bf[:].rearrange("p (q t) -> p q t", t=PACK),
+            in_=qv_ps[:].rearrange("p (t q) -> p q t", t=PACK), func=COPY)
+        nc.vector.tensor_copy(out=c_sb[:, cols(0)], in_=c_ps0[:])
+        q_codes = sb.tile([P, P], U32, name="q_codes", align_bytes=64)
+        q_plane = sb.tile([P, P], U8, name="q_plane", align_bytes=64)
+        nc.vector.quantize_mx(out=q_codes[:].bitcast(FP8X4), scales=q_plane[:], in_=qv_bf[:])
+
+        a_ps0 = scores("bank4", q_codes, q_plane, "keys", keys, FP8X4, 0)
+        a_ps1 = scores("bank5", q_codes, q_plane, "keys", keys, FP8X4, 1)
+        b_ps0 = scores("bank6", q_codes, q_plane, "notes", notes, FP4X4, 0)
+        b_ps1 = scores("bank7", q_codes, q_plane, "notes", notes, FP4X4, 1)
+
+        def entries(lst, half):
+            return lst[:, half * LIST_HALF:(half + 1) * LIST_HALF]
+
+        left = sb.tile([P, SLOTS], F32, name="left")
+        right = sb.tile([P, SLOTS], F32, name="right")
+        early_cd = sb.tile([P, SLOTS], F32, name="early_cd")
+        high0 = sb.tile([P, SLOTS], F32, name="high0")
+        shared = sb.tile([P, 2 * SLOTS - EARLY], F32, name="shared")
+        high1 = shared[:, 0:SLOTS]
+        r = shared[:, SLOTS - EARLY:]
+        lo, hi = slice(0, HALF), slice(HALF, 2 * HALF)
+        mid = slice(HALF // 2, HALF // 2 + HALF)
+
+        nc.scalar.activation(out=c_sb[:, cols(1)], in_=c_ps1[:], func=COPY)
+        nc.vector.tensor_copy(out=d_sb[:, cols(0)], in_=d_ps0[:])
+        nc.scalar.activation(out=early_cd[:, lo], in_=c_sb[:].indirect(entries(list3, 0)), func=COPY)
+        nc.vector.tensor_copy(out=d_sb[:, cols(1)], in_=d_ps1[:])
+        nc.scalar.activation(out=a_sb[:, cols(0)], in_=a_ps0[:], func=COPY)
+        nc.vector.tensor_copy(out=a_sb[:, cols(1)], in_=a_ps1[:])
+        nc.scalar.activation(out=b_sb[:, cols(0)], in_=b_ps0[:], func=COPY)
+        nc.vector.tensor_copy(out=b_sb[:, cols(1)], in_=b_ps1[:])
+        nc.scalar.activation(out=early_cd[:, hi], in_=d_sb[:].indirect(entries(list4, 0)), func=COPY)
+        nc.vector.tensor_copy(out=left[:, mid], in_=a_sb[:].indirect(entries(list1, 0)))
+        nc.scalar.activation(out=right[:, mid], in_=b_sb[:].indirect(entries(list2, 0)), func=COPY)
+        nc.vector.tensor_tensor(high0[:, hi], early_cd[:, lo], early_cd[:, hi], ALU.max)
+        nc.vector.tensor_tensor(high0[:, lo], left[:, mid], right[:, mid], ALU.max)
+        nc.vector.tensor_tensor(r[:, lo], high0[:, lo], high0[:, hi], ALU.min)
+
+        nc.scalar.activation(out=left[:, lo], in_=a_sb[:].indirect(entries(list1, 1)), func=COPY)
+        nc.scalar.activation(out=right[:, lo], in_=b_sb[:].indirect(entries(list2, 1)), func=COPY)
+        nc.scalar.activation(out=left[:, hi], in_=c_sb[:].indirect(entries(list3, 1)), func=COPY)
+        nc.scalar.activation(out=right[:, hi], in_=d_sb[:].indirect(entries(list4, 1)), func=COPY)
+
+        nc.vector.tensor_copy(out=f1[:].indirect(entries(list1, 0)), in_=r[:, lo])
+        nc.vector.tensor_copy(out=f2[:].indirect(list4[:, 0:EARLY // 16]), in_=r[:, 0:EARLY])
+        nc.vector.tensor_tensor(high1, left[:], right[:], ALU.max)
+        nc.vector.tensor_tensor(r[:, hi], high1[:, lo], high1[:, hi], ALU.min)
+        nc.vector.tensor_copy(out=f1[:].indirect(entries(list1, 1)), in_=r[:, hi])
+        nc.vector.tensor_copy(out=f2[:].indirect(list4[:, EARLY // 16:]), in_=r[:, EARLY:])
+
+        aa = sb.tile([P, COLS], F32, name="aa")
+        nc.gpsimd.tensor_tensor(aa[:], a_sb[:], f1[:], ALU.subtract)
+        g5 = sb.tile([P, SLOTS], F32, name="g5")
+        nc.scalar.activation(out=g5[:], in_=aa[:].indirect(list5[:]), func=COPY)
+
+        dd = sb.tile([P, COLS], F32, name="dd")
+        nc.vector.tensor_tensor(dd[:, cols(0)], d_ps0[:], f2[:, cols(0)], ALU.add)
+        nc.vector.tensor_tensor(dd[:, cols(1)], d_ps1[:], f2[:, cols(1)], ALU.add)
+        y = sb.tile([P, SLOTS], F32, name="y")
+        for half, part in enumerate((lo, hi)):
+            nc.vector.tensor_tensor(y[:, part], dd[:].indirect(entries(list6, half)), g5[:, part], ALU.add)
+            nc.sync.dma_start(out=out[:, part], in_=y[:, part])

@@ -15,13 +15,18 @@ COPY = mybir.ActivationFunctionType.Copy
 
 P = 128
 PACK = 4
-KDIM = 512
+KDIM = P * PACK
+BLOCKS = 16
+QUADRANT = 32
+LINE = 4
 COLS = 1024
-SLOTS = 512
 BANK = 512
+SLOTS = 512
+PER_COLUMN = 16
 HALF = SLOTS // 2
-LIST_HALF = HALF // 16
-EARLY = 128
+PIECE = SLOTS // 4
+VECTOR_COLS = 832
+ALIGN = 64
 
 FLOPS = 603979776
 
@@ -43,16 +48,19 @@ def tile_attend_quartet_madefour_kernel(
         for name, src in scale_inputs:
             start_of[name] = width
             width = width + src.shape[2]
-        wq_rows = sb.tile([P, KDIM], U8, name="wq_rows", align_bytes=64)
+        wq_rows = sb.tile([P, KDIM], U8, name="wq_rows", align_bytes=ALIGN)
         nc.vector.memset(wq_rows[:].bitcast(I32), 0)
-        staged = sb.tile([P, width], U8, name="staged", align_bytes=64)
-        planes = sb.tile([P, width], U8, name="planes", align_bytes=64)
-        for i, (name, src) in enumerate(scale_inputs):
-            queue = nc.scalar if i < 3 else nc.sync
-            c0 = start_of[name]
-            rows = wq_rows[0:16, :] if name == "wq" else staged[0:16, c0:c0 + src.shape[2]]
+        staged = sb.tile([P, width], U8, name="staged", align_bytes=ALIGN)
+        cut = start_of["keys"]
+        state_planes = sb.tile([P, cut], U8, name="state_planes", align_bytes=ALIGN)
+        query_planes = sb.tile([P, width - cut], U8, name="query_planes", align_bytes=ALIGN)
+        for name, src in scale_inputs:
+            queue = nc.sync if name in ("wq", "notes") else nc.scalar
+            first = start_of[name]
+            rows = wq_rows[0:BLOCKS, :] if name == "wq" else staged[0:BLOCKS, first:first + src.shape[2]]
             queue.dma_start(out=rows.bitcast(I32), in_=src[0].bitcast(I32))
-        nc.vector.memset(planes[:].bitcast(I32), 0)
+        nc.vector.memset(state_planes[:].bitcast(I32), 0)
+        nc.vector.memset(query_planes[:].bitcast(I32), 0)
         nc.vector.tensor_copy(
             out=staged[:, 0:KDIM].rearrange("p (t m) -> p t m", t=PACK),
             in_=wq_rows[:].rearrange("p (m t) -> p t m", t=PACK))
@@ -60,24 +68,28 @@ def tile_attend_quartet_madefour_kernel(
         states_raw = sb.tile([P, PACK, P], F32, name="states_raw")
         nc.sync.dma_start(out=states_raw[:], in_=states.rearrange("(p j) q -> p j q", j=PACK))
 
-        def load_words(name, src, queue=nc.sync):
-            words = sb.tile([P, src.shape[1]], U8, name=name, align_bytes=64)
-            queue.dma_start(out=words[:].bitcast(I32), in_=src.bitcast(I32))
+        def load_words(name, src):
+            words = sb.tile([P, src.shape[1]], U8, name=name, align_bytes=ALIGN)
+            nc.sync.dma_start(out=words[:].bitcast(I32), in_=src.bitcast(I32))
             return words
 
         def load_list(name, src):
-            lst = sb.tile([P, SLOTS // 16], U16, name=name)
+            lst = sb.tile([P, SLOTS // PER_COLUMN], U16, name=name)
             nc.sync.dma_start(lst[:], src)
             return lst
+
+        def spread_rows(planes, columns):
+            for j in range(PACK):
+                nc.sync.dma_start(out=planes[j:P:QUADRANT, :].bitcast(I32),
+                                  in_=staged[j:BLOCKS:PACK, columns].bitcast(I32))
 
         wq_raw = load_words("wq_raw", wq_words[0].rearrange("p n t -> p (n t)"))
         users = load_words("users", users_words[0].rearrange("p n t -> p (n t)"))
         list3 = load_list("list3", offs3)
-        for quad in range(4):
-            nc.sync.dma_start(out=planes[32 * quad:32 * quad + 4, :].bitcast(I32),
-                              in_=staged[4 * quad:4 * quad + 4, :].bitcast(I32))
+        spread_rows(state_planes, slice(0, cut))
         shelves = load_words("shelves", shelves_words[0])
         keys = load_words("keys", keys_words[0].rearrange("p n t -> p (n t)"))
+        spread_rows(query_planes, slice(cut, width))
         notes = load_words("notes", notes_words[0])
         list4 = load_list("list4", offs4)
         list1 = load_list("list1", offs)
@@ -85,115 +97,140 @@ def tile_attend_quartet_madefour_kernel(
         list5 = load_list("list5", offs5)
         list6 = load_list("list6", offs6)
 
-        f1 = sb.tile([P, COLS], F32, name="f1")
-        f2 = sb.tile([P, COLS], F32, name="f2")
+        states_bf = sb.tile([P, P * PACK], BF16, name="states_bf", align_bytes=ALIGN)
+        nc.scalar.activation(
+            out=states_bf[:].rearrange("p (c i j) -> p c j i", i=LINE, j=PACK),
+            in_=states_raw[:].rearrange("p j (c i) -> p c j i", i=LINE), func=COPY)
+        wq_dealt = sb.tile([P, KDIM], U32, name="wq_dealt", align_bytes=ALIGN)
+        nc.vector.tensor_copy(
+            out=wq_dealt[:].rearrange("p (t c i) -> p c t i", t=PACK, i=LINE),
+            in_=wq_raw[:].bitcast(U32).rearrange("p (c i t) -> p c t i", t=PACK, i=LINE))
+        s_codes = sb.tile([P, P], U32, name="s_codes", align_bytes=ALIGN)
+        s_plane = sb.tile([P, P], U8, name="s_plane", align_bytes=ALIGN)
+        nc.vector.quantize_mx(out=s_codes[:].bitcast(FP8X4), scales=s_plane[:], in_=states_bf[:])
+
+        f1 = sb.tile([P, COLS], F32, name="f1", tag="wq_raw", align_bytes=ALIGN)
+        f2 = sb.tile([P, COLS], F32, name="f2", tag="states_bf", align_bytes=ALIGN)
         nc.vector.memset(f1[:], 0.0)
         nc.vector.memset(f2[:], 0.0)
 
-        states_bf = sb.tile([P, P * PACK], BF16, name="states_bf", align_bytes=64)
-        nc.scalar.activation(
-            out=states_bf[:].rearrange("p (c i j) -> p c j i", i=4, j=PACK),
-            in_=states_raw[:].rearrange("p j (c i) -> p c j i", i=4), func=COPY)
-        wq_dealt = sb.tile([P, KDIM], U32, name="wq_dealt", align_bytes=64)
-        nc.vector.tensor_copy(
-            out=wq_dealt[:].rearrange("p (t b i) -> p b t i", t=PACK, i=4),
-            in_=wq_raw[:].bitcast(U32).rearrange("p (b i t) -> p b t i", t=PACK, i=4))
-        s_codes = sb.tile([P, P], U32, name="s_codes", align_bytes=64)
-        s_plane = sb.tile([P, P], U8, name="s_plane", align_bytes=64)
-        nc.vector.quantize_mx(out=s_codes[:].bitcast(FP8X4), scales=s_plane[:], in_=states_bf[:])
-
-        def scores(tag, codes, plane, name, words, dtype, half):
-            bank = ps.tile([P, BANK], F32, name=f"{name}{half}", tag=tag)
+        def scores(bank_tag, codes, plane, name, words, dtype, half):
+            bank = ps.tile([P, BANK], F32, name=f"{name}{half}", tag=bank_tag)
             nbytes = words.shape[1] // 2
-            c0 = start_of[name] + half * BANK
+            first = start_of[name] + half * BANK
+            if first < cut:
+                table_plane = state_planes[:, first:first + BANK]
+            else:
+                table_plane = query_planes[:, first - cut:first - cut + BANK]
             nc.tensor.matmul_mx(
                 out=bank[:], lhsT=codes[:].bitcast(FP8X4), lhsT_scale=plane[:],
                 rhs=words[:, half * nbytes:(half + 1) * nbytes].bitcast(dtype),
-                rhs_scale=planes[:, c0:c0 + BANK], start=True, stop=True)
+                rhs_scale=table_plane, start=True, stop=True)
             return bank
 
-        def cols(half):
+        def bank_cols(half):
             return slice(half * BANK, (half + 1) * BANK)
 
         a_sb = sb.tile([P, COLS], F32, name="a_sb")
         b_sb = sb.tile([P, COLS], F32, name="b_sb")
         c_sb = sb.tile([P, COLS], F32, name="c_sb")
-        d_sb = sb.tile([P, COLS], F32, name="d_sb")
 
         qv_ps = ps.tile([P, BANK], F32, name="qv_ps", tag="bank7")
         for t in range(PACK):
             nc.tensor.matmul_mx(
                 out=qv_ps[:, t * P:(t + 1) * P],
-                lhsT=wq_dealt[:, t * P:(t + 1) * P].bitcast(FP8X4), lhsT_scale=planes[:, t * P:(t + 1) * P],
+                lhsT=wq_dealt[:, t * P:(t + 1) * P].bitcast(FP8X4), lhsT_scale=state_planes[:, t * P:(t + 1) * P],
                 rhs=s_codes[:].bitcast(FP8X4), rhs_scale=s_plane[:], start=True, stop=True)
         c_ps0 = scores("bank0", s_codes, s_plane, "users", users, FP8X4, 0)
         c_ps1 = scores("bank1", s_codes, s_plane, "users", users, FP8X4, 1)
         d_ps0 = scores("bank2", s_codes, s_plane, "shelves", shelves, FP4X4, 0)
         d_ps1 = scores("bank3", s_codes, s_plane, "shelves", shelves, FP4X4, 1)
 
-        qv_bf = sb.tile([P, P * PACK], BF16, name="qv_bf", align_bytes=64)
+        qv_bf = sb.tile([P, P * PACK], BF16, name="qv_bf", align_bytes=ALIGN)
         nc.scalar.activation(
             out=qv_bf[:].rearrange("p (q t) -> p q t", t=PACK),
             in_=qv_ps[:].rearrange("p (t q) -> p q t", t=PACK), func=COPY)
-        nc.vector.tensor_copy(out=c_sb[:, cols(0)], in_=c_ps0[:])
-        q_codes = sb.tile([P, P], U32, name="q_codes", align_bytes=64)
-        q_plane = sb.tile([P, P], U8, name="q_plane", align_bytes=64)
+        nc.vector.tensor_copy(out=c_sb[:, bank_cols(0)], in_=c_ps0[:])
+        q_codes = sb.tile([P, P], U32, name="q_codes", align_bytes=ALIGN)
+        q_plane = sb.tile([P, P], U8, name="q_plane", align_bytes=ALIGN)
         nc.vector.quantize_mx(out=q_codes[:].bitcast(FP8X4), scales=q_plane[:], in_=qv_bf[:])
+
+        d_sb = sb.tile([P, COLS], F32, name="d_sb", tag="qv_bf", align_bytes=ALIGN)
 
         a_ps0 = scores("bank4", q_codes, q_plane, "keys", keys, FP8X4, 0)
         a_ps1 = scores("bank5", q_codes, q_plane, "keys", keys, FP8X4, 1)
         b_ps0 = scores("bank6", q_codes, q_plane, "notes", notes, FP4X4, 0)
         b_ps1 = scores("bank7", q_codes, q_plane, "notes", notes, FP4X4, 1)
 
-        def entries(lst, half):
-            return lst[:, half * LIST_HALF:(half + 1) * LIST_HALF]
+        def entries(lst, slots):
+            return lst[:, slots.start // PER_COLUMN:slots.stop // PER_COLUMN]
 
-        left = sb.tile([P, SLOTS], F32, name="left")
-        right = sb.tile([P, SLOTS], F32, name="right")
-        early_cd = sb.tile([P, SLOTS], F32, name="early_cd")
-        high0 = sb.tile([P, SLOTS], F32, name="high0")
-        shared = sb.tile([P, 2 * SLOTS - EARLY], F32, name="shared")
-        high1 = shared[:, 0:SLOTS]
-        r = shared[:, SLOTS - EARLY:]
-        lo, hi = slice(0, HALF), slice(HALF, 2 * HALF)
-        mid = slice(HALF // 2, HALF // 2 + HALF)
+        def piece(i):
+            return slice(i * PIECE, (i + 1) * PIECE)
 
-        nc.scalar.activation(out=c_sb[:, cols(1)], in_=c_ps1[:], func=COPY)
-        nc.vector.tensor_copy(out=d_sb[:, cols(0)], in_=d_ps0[:])
-        nc.scalar.activation(out=early_cd[:, lo], in_=c_sb[:].indirect(entries(list3, 0)), func=COPY)
-        nc.vector.tensor_copy(out=d_sb[:, cols(1)], in_=d_ps1[:])
-        nc.scalar.activation(out=a_sb[:, cols(0)], in_=a_ps0[:], func=COPY)
-        nc.vector.tensor_copy(out=a_sb[:, cols(1)], in_=a_ps1[:])
-        nc.scalar.activation(out=b_sb[:, cols(0)], in_=b_ps0[:], func=COPY)
-        nc.vector.tensor_copy(out=b_sb[:, cols(1)], in_=b_ps1[:])
-        nc.scalar.activation(out=early_cd[:, hi], in_=d_sb[:].indirect(entries(list4, 0)), func=COPY)
-        nc.vector.tensor_copy(out=left[:, mid], in_=a_sb[:].indirect(entries(list1, 0)))
-        nc.scalar.activation(out=right[:, mid], in_=b_sb[:].indirect(entries(list2, 0)), func=COPY)
-        nc.vector.tensor_tensor(high0[:, hi], early_cd[:, lo], early_cd[:, hi], ALU.max)
-        nc.vector.tensor_tensor(high0[:, lo], left[:, mid], right[:, mid], ALU.max)
-        nc.vector.tensor_tensor(r[:, lo], high0[:, lo], high0[:, hi], ALU.min)
+        lo, hi = slice(0, HALF), slice(HALF, SLOTS)
+        mid = slice(PIECE, PIECE + HALF)
+        picked_ac = sb.tile([P, SLOTS], F32, name="picked_ac")
+        picked_bd = sb.tile([P, SLOTS], F32, name="picked_bd")
+        c_first = sb.tile([P, HALF], F32, name="c_first")
+        d_first = sb.tile([P, HALF], F32, name="d_first", tag="q_codes", align_bytes=ALIGN)
+        high_first = sb.tile([P, SLOTS], F32, name="high_first")
+        high_second = sb.tile([P, SLOTS], F32, name="high_second")
+        r_rest = sb.tile([P, SLOTS - PIECE], F32, name="r_rest")
+        r_first = high_second[:, HALF + PIECE // 2:HALF + PIECE // 2 + PIECE]
+        r = [r_first] + [r_rest[:, piece(i)] for i in range(3)]
 
-        nc.scalar.activation(out=left[:, lo], in_=a_sb[:].indirect(entries(list1, 1)), func=COPY)
-        nc.scalar.activation(out=right[:, lo], in_=b_sb[:].indirect(entries(list2, 1)), func=COPY)
-        nc.scalar.activation(out=left[:, hi], in_=c_sb[:].indirect(entries(list3, 1)), func=COPY)
-        nc.scalar.activation(out=right[:, hi], in_=d_sb[:].indirect(entries(list4, 1)), func=COPY)
+        nc.scalar.activation(out=c_sb[:, bank_cols(1)], in_=c_ps1[:], func=COPY)
+        nc.vector.tensor_copy(out=d_sb[:, bank_cols(0)], in_=d_ps0[:])
+        nc.scalar.activation(out=c_first[:], in_=c_sb[:].indirect(entries(list3, lo)), func=COPY)
+        nc.vector.tensor_copy(out=d_sb[:, bank_cols(1)], in_=d_ps1[:])
+        nc.scalar.activation(out=a_sb[:, bank_cols(0)], in_=a_ps0[:], func=COPY)
+        nc.vector.tensor_copy(out=a_sb[:, bank_cols(1)], in_=a_ps1[:])
+        nc.scalar.activation(out=b_sb[:, bank_cols(0)], in_=b_ps0[:], func=COPY)
+        nc.vector.tensor_copy(out=b_sb[:, bank_cols(1)], in_=b_ps1[:])
+        nc.scalar.activation(out=d_first[:], in_=d_sb[:].indirect(entries(list4, lo)), func=COPY)
+        nc.vector.tensor_copy(out=picked_ac[:, mid], in_=a_sb[:].indirect(entries(list1, lo)))
+        nc.scalar.activation(out=picked_bd[:, mid], in_=b_sb[:].indirect(entries(list2, lo)), func=COPY)
+        nc.vector.tensor_tensor(high_first[:, hi], c_first[:], d_first[:], ALU.max)
+        for i in range(2):
+            nc.vector.tensor_tensor(
+                high_first[:, piece(i)], picked_ac[:, piece(i + 1)], picked_bd[:, piece(i + 1)], ALU.max)
+        for i in range(2):
+            nc.vector.tensor_tensor(r[i], high_first[:, piece(i)], high_first[:, piece(i + 2)], ALU.min)
 
-        nc.vector.tensor_copy(out=f1[:].indirect(entries(list1, 0)), in_=r[:, lo])
-        nc.vector.tensor_copy(out=f2[:].indirect(list4[:, 0:EARLY // 16]), in_=r[:, 0:EARLY])
-        nc.vector.tensor_tensor(high1, left[:], right[:], ALU.max)
-        nc.vector.tensor_tensor(r[:, hi], high1[:, lo], high1[:, hi], ALU.min)
-        nc.vector.tensor_copy(out=f1[:].indirect(entries(list1, 1)), in_=r[:, hi])
-        nc.vector.tensor_copy(out=f2[:].indirect(list4[:, EARLY // 16:]), in_=r[:, EARLY:])
+        nc.scalar.activation(out=picked_ac[:, lo], in_=a_sb[:].indirect(entries(list1, hi)), func=COPY)
+        nc.scalar.activation(out=picked_bd[:, lo], in_=b_sb[:].indirect(entries(list2, hi)), func=COPY)
+        nc.scalar.activation(out=picked_ac[:, hi], in_=c_sb[:].indirect(entries(list3, hi)), func=COPY)
+        nc.scalar.activation(out=picked_bd[:, hi], in_=d_sb[:].indirect(entries(list4, hi)), func=COPY)
+        nc.vector.tensor_copy(out=f1[:].indirect(entries(list1, piece(0))), in_=r[0])
+        nc.vector.tensor_copy(out=f2[:].indirect(entries(list4, piece(0))), in_=r[0])
+        nc.vector.tensor_copy(out=f1[:].indirect(entries(list1, piece(1))), in_=r[1])
+
+        def both_parts(ap, i):
+            return ap.rearrange("p (s i c) -> p i s c", s=2, i=2)[:, i]
+
+        for i in range(2):
+            nc.vector.tensor_tensor(
+                both_parts(high_second[:], i), both_parts(picked_ac[:], i), both_parts(picked_bd[:], i), ALU.max)
+        for i in range(2):
+            nc.vector.tensor_tensor(r[i + 2], high_second[:, piece(i)], high_second[:, piece(i + 2)], ALU.min)
+        nc.vector.tensor_copy(out=f1[:].indirect(entries(list1, hi)), in_=r_rest[:, PIECE:])
+        nc.vector.tensor_copy(out=f2[:].indirect(entries(list4, slice(PIECE, SLOTS))), in_=r_rest[:])
 
         aa = sb.tile([P, COLS], F32, name="aa")
         nc.gpsimd.tensor_tensor(aa[:], a_sb[:], f1[:], ALU.subtract)
-        g5 = sb.tile([P, SLOTS], F32, name="g5")
-        nc.scalar.activation(out=g5[:], in_=aa[:].indirect(list5[:]), func=COPY)
+        aa_picked = sb.tile([P, SLOTS], F32, name="aa_picked")
+        for slots in (lo, hi):
+            nc.scalar.activation(out=aa_picked[:, slots], in_=aa[:].indirect(entries(list5, slots)), func=COPY)
 
         dd = sb.tile([P, COLS], F32, name="dd")
-        nc.vector.tensor_tensor(dd[:, cols(0)], d_ps0[:], f2[:, cols(0)], ALU.add)
-        nc.vector.tensor_tensor(dd[:, cols(1)], d_ps1[:], f2[:, cols(1)], ALU.add)
-        y = sb.tile([P, SLOTS], F32, name="y")
-        for half, part in enumerate((lo, hi)):
-            nc.vector.tensor_tensor(y[:, part], dd[:].indirect(entries(list6, half)), g5[:, part], ALU.add)
-            nc.sync.dma_start(out=out[:, part], in_=y[:, part])
+        nc.vector.tensor_tensor(dd[:, bank_cols(0)], d_ps0[:], f2[:, bank_cols(0)], ALU.add)
+        nc.vector.tensor_tensor(
+            dd[:, BANK:VECTOR_COLS], d_ps1[:, 0:VECTOR_COLS - BANK], f2[:, BANK:VECTOR_COLS], ALU.add)
+        nc.gpsimd.tensor_tensor(dd[:, VECTOR_COLS:], d_sb[:, VECTOR_COLS:], f2[:, VECTOR_COLS:], ALU.add)
+
+        result = sb.tile([P, SLOTS], F32, name="result")
+        for slots in (lo, hi):
+            nc.vector.tensor_tensor(
+                result[:, slots], dd[:].indirect(entries(list6, slots)), aa_picked[:, slots], ALU.add)
+            nc.sync.dma_start(out=out[:, slots], in_=result[:, slots])

from contextlib import ExitStack

import concourse.mybir as mybir

F32 = mybir.dt.float32
BF16 = mybir.dt.bfloat16
I32 = mybir.dt.int32
U32 = mybir.dt.uint32
U16 = mybir.dt.uint16
U8 = mybir.dt.uint8
FP8X4 = mybir.dt.float8_e4m3fn_x4
FP4X4 = mybir.dt.float4_e2m1fn_x4
ALU = mybir.AluOpType
COPY = mybir.ActivationFunctionType.Copy

P = 128
PACK = 4
KDIM = P * PACK
BLOCKS = 16
QUADRANT = 32
LINE = 4
COLS = 1024
BANK = 512
SLOTS = 512
PER_COLUMN = 16
HALF = SLOTS // 2
PIECE = SLOTS // 4
VECTOR_COLS = 832
ALIGN = 64

FLOPS = 603979776


def tile_attend_quartet_madefour_kernel(
    tc, states, wq_words, wq_scales, keys_words, keys_scales, notes_words, notes_scales,
    users_words, users_scales, shelves_words, shelves_scales,
    offs, offs2, offs3, offs4, offs5, offs6, out,
):
    nc = tc.nc
    with ExitStack() as ctx:
        sb = ctx.enter_context(tc.tile_pool(name="sb", bufs=1))
        ps = ctx.enter_context(tc.psum_pool(name="ps", bufs=1))

        scale_inputs = [("wq", wq_scales), ("users", users_scales), ("shelves", shelves_scales),
                        ("keys", keys_scales), ("notes", notes_scales)]
        start_of = {}
        width = 0
        for name, src in scale_inputs:
            start_of[name] = width
            width = width + src.shape[2]
        wq_rows = sb.tile([P, KDIM], U8, name="wq_rows", align_bytes=ALIGN)
        nc.vector.memset(wq_rows[:].bitcast(I32), 0)
        staged = sb.tile([P, width], U8, name="staged", align_bytes=ALIGN)
        cut = start_of["keys"]
        state_planes = sb.tile([P, cut], U8, name="state_planes", align_bytes=ALIGN)
        query_planes = sb.tile([P, width - cut], U8, name="query_planes", align_bytes=ALIGN)
        for name, src in scale_inputs:
            queue = nc.sync if name in ("wq", "notes") else nc.scalar
            first = start_of[name]
            rows = wq_rows[0:BLOCKS, :] if name == "wq" else staged[0:BLOCKS, first:first + src.shape[2]]
            queue.dma_start(out=rows.bitcast(I32), in_=src[0].bitcast(I32))
        nc.vector.memset(state_planes[:].bitcast(I32), 0)
        nc.vector.memset(query_planes[:].bitcast(I32), 0)
        nc.vector.tensor_copy(
            out=staged[:, 0:KDIM].rearrange("p (t m) -> p t m", t=PACK),
            in_=wq_rows[:].rearrange("p (m t) -> p t m", t=PACK))

        states_raw = sb.tile([P, PACK, P], F32, name="states_raw")
        nc.sync.dma_start(out=states_raw[:], in_=states.rearrange("(p j) q -> p j q", j=PACK))

        def load_words(name, src):
            words = sb.tile([P, src.shape[1]], U8, name=name, align_bytes=ALIGN)
            nc.sync.dma_start(out=words[:].bitcast(I32), in_=src.bitcast(I32))
            return words

        def load_list(name, src):
            lst = sb.tile([P, SLOTS // PER_COLUMN], U16, name=name)
            nc.sync.dma_start(lst[:], src)
            return lst

        def spread_rows(planes, columns):
            for j in range(PACK):
                nc.sync.dma_start(out=planes[j:P:QUADRANT, :].bitcast(I32),
                                  in_=staged[j:BLOCKS:PACK, columns].bitcast(I32))

        wq_raw = load_words("wq_raw", wq_words[0].rearrange("p n t -> p (n t)"))
        users = load_words("users", users_words[0].rearrange("p n t -> p (n t)"))
        list3 = load_list("list3", offs3)
        spread_rows(state_planes, slice(0, cut))
        shelves = load_words("shelves", shelves_words[0])
        keys = load_words("keys", keys_words[0].rearrange("p n t -> p (n t)"))
        spread_rows(query_planes, slice(cut, width))
        notes = load_words("notes", notes_words[0])
        list4 = load_list("list4", offs4)
        list1 = load_list("list1", offs)
        list2 = load_list("list2", offs2)
        list5 = load_list("list5", offs5)
        list6 = load_list("list6", offs6)

        states_bf = sb.tile([P, P * PACK], BF16, name="states_bf", align_bytes=ALIGN)
        nc.scalar.activation(
            out=states_bf[:].rearrange("p (c i j) -> p c j i", i=LINE, j=PACK),
            in_=states_raw[:].rearrange("p j (c i) -> p c j i", i=LINE), func=COPY)
        wq_dealt = sb.tile([P, KDIM], U32, name="wq_dealt", align_bytes=ALIGN)
        nc.vector.tensor_copy(
            out=wq_dealt[:].rearrange("p (t c i) -> p c t i", t=PACK, i=LINE),
            in_=wq_raw[:].bitcast(U32).rearrange("p (c i t) -> p c t i", t=PACK, i=LINE))
        s_codes = sb.tile([P, P], U32, name="s_codes", align_bytes=ALIGN)
        s_plane = sb.tile([P, P], U8, name="s_plane", align_bytes=ALIGN)
        nc.vector.quantize_mx(out=s_codes[:].bitcast(FP8X4), scales=s_plane[:], in_=states_bf[:])

        f1 = sb.tile([P, COLS], F32, name="f1", tag="wq_raw", align_bytes=ALIGN)
        f2 = sb.tile([P, COLS], F32, name="f2", tag="states_bf", align_bytes=ALIGN)
        nc.vector.memset(f1[:], 0.0)
        nc.vector.memset(f2[:], 0.0)

        def scores(bank_tag, codes, plane, name, words, dtype, half):
            bank = ps.tile([P, BANK], F32, name=f"{name}{half}", tag=bank_tag)
            nbytes = words.shape[1] // 2
            first = start_of[name] + half * BANK
            if first < cut:
                table_plane = state_planes[:, first:first + BANK]
            else:
                table_plane = query_planes[:, first - cut:first - cut + BANK]
            nc.tensor.matmul_mx(
                out=bank[:], lhsT=codes[:].bitcast(FP8X4), lhsT_scale=plane[:],
                rhs=words[:, half * nbytes:(half + 1) * nbytes].bitcast(dtype),
                rhs_scale=table_plane, start=True, stop=True)
            return bank

        def bank_cols(half):
            return slice(half * BANK, (half + 1) * BANK)

        a_sb = sb.tile([P, COLS], F32, name="a_sb")
        b_sb = sb.tile([P, COLS], F32, name="b_sb")
        c_sb = sb.tile([P, COLS], F32, name="c_sb")

        qv_ps = ps.tile([P, BANK], F32, name="qv_ps", tag="bank7")
        for t in range(PACK):
            nc.tensor.matmul_mx(
                out=qv_ps[:, t * P:(t + 1) * P],
                lhsT=wq_dealt[:, t * P:(t + 1) * P].bitcast(FP8X4), lhsT_scale=state_planes[:, t * P:(t + 1) * P],
                rhs=s_codes[:].bitcast(FP8X4), rhs_scale=s_plane[:], start=True, stop=True)
        c_ps0 = scores("bank0", s_codes, s_plane, "users", users, FP8X4, 0)
        c_ps1 = scores("bank1", s_codes, s_plane, "users", users, FP8X4, 1)
        d_ps0 = scores("bank2", s_codes, s_plane, "shelves", shelves, FP4X4, 0)
        d_ps1 = scores("bank3", s_codes, s_plane, "shelves", shelves, FP4X4, 1)

        qv_bf = sb.tile([P, P * PACK], BF16, name="qv_bf", align_bytes=ALIGN)
        nc.scalar.activation(
            out=qv_bf[:].rearrange("p (q t) -> p q t", t=PACK),
            in_=qv_ps[:].rearrange("p (t q) -> p q t", t=PACK), func=COPY)
        nc.vector.tensor_copy(out=c_sb[:, bank_cols(0)], in_=c_ps0[:])
        q_codes = sb.tile([P, P], U32, name="q_codes", align_bytes=ALIGN)
        q_plane = sb.tile([P, P], U8, name="q_plane", align_bytes=ALIGN)
        nc.vector.quantize_mx(out=q_codes[:].bitcast(FP8X4), scales=q_plane[:], in_=qv_bf[:])

        d_sb = sb.tile([P, COLS], F32, name="d_sb", tag="qv_bf", align_bytes=ALIGN)

        a_ps0 = scores("bank4", q_codes, q_plane, "keys", keys, FP8X4, 0)
        a_ps1 = scores("bank5", q_codes, q_plane, "keys", keys, FP8X4, 1)
        b_ps0 = scores("bank6", q_codes, q_plane, "notes", notes, FP4X4, 0)
        b_ps1 = scores("bank7", q_codes, q_plane, "notes", notes, FP4X4, 1)

        def entries(lst, slots):
            return lst[:, slots.start // PER_COLUMN:slots.stop // PER_COLUMN]

        def piece(i):
            return slice(i * PIECE, (i + 1) * PIECE)

        lo, hi = slice(0, HALF), slice(HALF, SLOTS)
        mid = slice(PIECE, PIECE + HALF)
        picked_ac = sb.tile([P, SLOTS], F32, name="picked_ac")
        picked_bd = sb.tile([P, SLOTS], F32, name="picked_bd")
        c_first = sb.tile([P, HALF], F32, name="c_first")
        d_first = sb.tile([P, HALF], F32, name="d_first", tag="q_codes", align_bytes=ALIGN)
        high_first = sb.tile([P, SLOTS], F32, name="high_first")
        high_second = sb.tile([P, SLOTS], F32, name="high_second")
        r_rest = sb.tile([P, SLOTS - PIECE], F32, name="r_rest")
        r_first = high_second[:, HALF + PIECE // 2:HALF + PIECE // 2 + PIECE]
        r = [r_first] + [r_rest[:, piece(i)] for i in range(3)]

        nc.scalar.activation(out=c_sb[:, bank_cols(1)], in_=c_ps1[:], func=COPY)
        nc.vector.tensor_copy(out=d_sb[:, bank_cols(0)], in_=d_ps0[:])
        nc.scalar.activation(out=c_first[:], in_=c_sb[:].indirect(entries(list3, lo)), func=COPY)
        nc.vector.tensor_copy(out=d_sb[:, bank_cols(1)], in_=d_ps1[:])
        nc.scalar.activation(out=a_sb[:, bank_cols(0)], in_=a_ps0[:], func=COPY)
        nc.vector.tensor_copy(out=a_sb[:, bank_cols(1)], in_=a_ps1[:])
        nc.scalar.activation(out=b_sb[:, bank_cols(0)], in_=b_ps0[:], func=COPY)
        nc.vector.tensor_copy(out=b_sb[:, bank_cols(1)], in_=b_ps1[:])
        nc.scalar.activation(out=d_first[:], in_=d_sb[:].indirect(entries(list4, lo)), func=COPY)
        nc.vector.tensor_copy(out=picked_ac[:, mid], in_=a_sb[:].indirect(entries(list1, lo)))
        nc.scalar.activation(out=picked_bd[:, mid], in_=b_sb[:].indirect(entries(list2, lo)), func=COPY)
        nc.vector.tensor_tensor(high_first[:, hi], c_first[:], d_first[:], ALU.max)
        for i in range(2):
            nc.vector.tensor_tensor(
                high_first[:, piece(i)], picked_ac[:, piece(i + 1)], picked_bd[:, piece(i + 1)], ALU.max)
        for i in range(2):
            nc.vector.tensor_tensor(r[i], high_first[:, piece(i)], high_first[:, piece(i + 2)], ALU.min)

        nc.scalar.activation(out=picked_ac[:, lo], in_=a_sb[:].indirect(entries(list1, hi)), func=COPY)
        nc.scalar.activation(out=picked_bd[:, lo], in_=b_sb[:].indirect(entries(list2, hi)), func=COPY)
        nc.scalar.activation(out=picked_ac[:, hi], in_=c_sb[:].indirect(entries(list3, hi)), func=COPY)
        nc.scalar.activation(out=picked_bd[:, hi], in_=d_sb[:].indirect(entries(list4, hi)), func=COPY)
        nc.vector.tensor_copy(out=f1[:].indirect(entries(list1, piece(0))), in_=r[0])
        nc.vector.tensor_copy(out=f2[:].indirect(entries(list4, piece(0))), in_=r[0])
        nc.vector.tensor_copy(out=f1[:].indirect(entries(list1, piece(1))), in_=r[1])

        def both_parts(ap, i):
            return ap.rearrange("p (s i c) -> p i s c", s=2, i=2)[:, i]

        for i in range(2):
            nc.vector.tensor_tensor(
                both_parts(high_second[:], i), both_parts(picked_ac[:], i), both_parts(picked_bd[:], i), ALU.max)
        for i in range(2):
            nc.vector.tensor_tensor(r[i + 2], high_second[:, piece(i)], high_second[:, piece(i + 2)], ALU.min)
        nc.vector.tensor_copy(out=f1[:].indirect(entries(list1, hi)), in_=r_rest[:, PIECE:])
        nc.vector.tensor_copy(out=f2[:].indirect(entries(list4, slice(PIECE, SLOTS))), in_=r_rest[:])

        aa = sb.tile([P, COLS], F32, name="aa")
        nc.gpsimd.tensor_tensor(aa[:], a_sb[:], f1[:], ALU.subtract)
        aa_picked = sb.tile([P, SLOTS], F32, name="aa_picked")
        for slots in (lo, hi):
            nc.scalar.activation(out=aa_picked[:, slots], in_=aa[:].indirect(entries(list5, slots)), func=COPY)

        dd = sb.tile([P, COLS], F32, name="dd")
        nc.vector.tensor_tensor(dd[:, bank_cols(0)], d_ps0[:], f2[:, bank_cols(0)], ALU.add)
        nc.vector.tensor_tensor(
            dd[:, BANK:VECTOR_COLS], d_ps1[:, 0:VECTOR_COLS - BANK], f2[:, BANK:VECTOR_COLS], ALU.add)
        nc.gpsimd.tensor_tensor(dd[:, VECTOR_COLS:], d_sb[:, VECTOR_COLS:], f2[:, VECTOR_COLS:], ALU.add)

        result = sb.tile([P, SLOTS], F32, name="result")
        for slots in (lo, hi):
            nc.vector.tensor_tensor(
                result[:, slots], dd[:].indirect(entries(list6, slots)), aa_picked[:, slots], ALU.add)
            nc.sync.dma_start(out=out[:, slots], in_=result[:, slots])
